import numpy as np
import ml_dtypes


def mxq(x, axis, fmt="e4m3"):
    dtype, down = {"e4m3": (ml_dtypes.float8_e4m3fn, 7), "e5m2": (ml_dtypes.float8_e5m2, 14)}[fmt]
    v = np.moveaxis(np.asarray(x, np.float32).astype(ml_dtypes.bfloat16).astype(np.float64), axis, -1)
    blocks = v.reshape(v.shape[:-1] + (-1, 32))
    amax = np.abs(blocks).max(-1, keepdims=True)
    byte = np.maximum(np.where(amax > 0, np.frexp(amax)[1] - 1 + 127, 0) - down, 1)
    scale = np.exp2(byte - 127.0)
    codes = (blocks / scale).astype(np.float32).astype(dtype).astype(np.float64)
    return np.moveaxis((codes * scale).reshape(v.shape), -1, axis)


WIDE = False


def mx_kscale(k):
    if not WIDE:
        return np.ones(k)
    levels = np.array([10, -10, 5, -5, 0])
    if k % 512:
        return np.exp2(np.random.permutation(np.resize(levels, k // 32))).repeat(32)
    a = np.empty((k // 512, 16))
    for p in range(k // 512):
        a[p, :8] = np.random.permutation(np.resize(levels, 8))
        for g in range(8):
            far = levels[np.abs(levels - a[p, g]) >= 10]
            a[p, g + 8] = far[np.random.randint(len(far))]
    return np.exp2(a.ravel()).repeat(32)


BF16 = ml_dtypes.bfloat16


def bf(x):
    return np.asarray(x, np.float32).astype(BF16)


def f64(x):
    return np.asarray(x).astype(np.float64)


N, K, H = 1024, 1024, 512
G = 3 * H


def sigmoid(v):
    return 1.0 / (1.0 + np.exp(-v))


def draw0():
    s = mx_kscale(K)
    u = mx_kscale(N)
    return {
        "z": bf(np.random.standard_normal((N, K))),
        "c": bf(np.random.standard_normal((N, H))),
        "w": bf(np.random.standard_normal((K, G)) * (1.2 / np.sqrt(K)) / s[:, None]),
        "b": bf(np.random.standard_normal(G) * 0.4),
        "a": bf((1.0 + 0.1 * np.random.standard_normal(K)) * s),
        "r": bf((1.0 + 0.1 * np.random.standard_normal(N)) * u),
        "dh_new": bf(np.random.standard_normal((N, H)) / u[:, None]),
    }


def gate_preactivations(z, w, b, a):
    za = z * a[None, :]
    return (mxq(za, 1, "e4m3") @ mxq(w, 0, "e4m3")) + b[None, :]


def gate_deltas(p, c, dh_new):
    h = c.shape[1]
    pf = p[:, :h]
    pg = p[:, h:2 * h]
    po = p[:, 2 * h:]
    f = sigmoid(pf)
    g = np.tanh(pg)
    o = sigmoid(po)
    tc = np.tanh(f * c + (1.0 - f) * g)
    dct = dh_new * o * (1.0 - tc * tc)
    dpf = dct * (c - g) * f * (1.0 - f)
    dpg = dct * (1.0 - f) * (1.0 - g * g)
    dpo = dh_new * tc * o * (1.0 - o)
    return np.concatenate([dpf, dpg, dpo], axis=-1)


def core(z, c, w, b, a, r, dh_new):
    z, c, w, b, a, r, dh_new = f64(z), f64(c), f64(w), f64(b), f64(a), f64(r), f64(dh_new)
    p = gate_preactivations(z, w, b, a)
    delta = gate_deltas(p, c, dh_new)
    zr = z * r[:, None]
    return mxq(zr, 0, "e4m3").T @ mxq(delta, 0, "e4m3")


def e4m3fn_bytes(y):
    return np.clip(np.asarray(y, np.float64), -448.0, 448.0).astype(np.float32).astype(ml_dtypes.float8_e4m3fn).view(np.uint8)


def e4m3fn_values(b):
    return np.asarray(b, np.uint8).view(ml_dtypes.float8_e4m3fn).astype(np.float64)


def setup_inputs():
    d = draw0()
    x0 = np.asarray(d['w']).astype(np.float64)
    s = (np.max(np.abs(x0), axis=(1,), keepdims=True) / 448.0).astype(np.float32)
    out = {}
    for k, v in d.items():
        if k == 'w':
            out['w_bytes'] = e4m3fn_bytes(x0 / s.astype(np.float64))
            out['w_scale'] = s
        else:
            out[k] = v
    return out


def reference(z, c, w_bytes, w_scale, b, a, r, dh_new):
    return core(z, c, e4m3fn_values(w_bytes) * w_scale.astype(np.float64), b, a, r, dh_new)

@@ -1,0 +1,488 @@
+from contextlib import ExitStack
+
+import concourse.mybir as mybir
+from concourse.masks import make_identity
+
+N, K, H = 1024, 1024, 512
+GATES = 3
+FLOPS = 2 * 2 * N * K * GATES * H
+
+F32 = mybir.dt.float32
+BF16 = mybir.dt.bfloat16
+U32 = mybir.dt.uint32
+U8 = mybir.dt.uint8
+FP8 = mybir.dt.float8_e4m3fn
+FP8X4 = mybir.dt.float8_e4m3fn_x4
+ALU = mybir.AluOpType
+ACT = mybir.ActivationFunctionType
+
+P = 128
+PACK = 4
+PASS = P * PACK
+PASSES = 2
+TILES = H // P
+UNITS = TILES * PASSES
+GATE_F, GATE_G, GATE_O = 0, 1, 2
+WIDEN_SPANS = [(0, 1), (1, 1), (2, 2)]
+
+
+def tile_coupledlstmfoldedweightgradient_kernel(tc, z, c, w_bytes, w_scale, b, a, r, dh_new, out):
+    nc = tc.nc
+    with ExitStack() as ctx:
+        keep = ctx.enter_context(tc.tile_pool(name="keep", bufs=1))
+        work = ctx.enter_context(tc.tile_pool(name="work", bufs=2))
+        psum = ctx.enter_context(tc.psum_pool(name="psum", bufs=1))
+        ctx.enter_context(tc.manual_schedule())
+
+        def quantize(codes, scales, values):
+            nc.vector.quantize_mx(out=codes.bitcast(FP8X4), scales=scales, in_=values)
+
+        def mx_tiles(pool, name, width, bufs=None):
+            codes = pool.tile([P, width], U32, name=name + "_codes", bufs=bufs, align_bytes=64)
+            scales = pool.tile([P, width], U8, name=name + "_scales", bufs=bufs, align_bytes=64)
+            return codes, scales
+
+        def matmul_mx(acc, lhs, lhs_cols, rhs, rhs_cols, start, stop):
+            nc.tensor.matmul_mx(
+                out=acc, lhsT=lhs[0][:, lhs_cols].bitcast(FP8X4), lhsT_scale=lhs[1][:, lhs_cols],
+                rhs=rhs[0][:, rhs_cols].bitcast(FP8X4), rhs_scale=rhs[1][:, rhs_cols], start=start, stop=stop)
+
+        def spare_bank(shape, dtype, borrow=None):
+            if borrow:
+                return psum.tile(shape, dtype, name=borrow)
+            return psum.tile(shape, dtype, name="spare_bank", bufs=2)
+
+        ident_f32 = keep.tile([P, P], F32)
+        make_identity(nc, ident_f32[:])
+        ident_bf16 = keep.tile([P, P], BF16)
+        make_identity(nc, ident_bf16[:])
+        bias_rows = keep.tile([P, P], BF16)
+        nc.gpsimd.memset(bias_rows[:], 0.0)
+        warm_in = keep.tile([P, 1], F32)
+        nc.vector.memset(warm_in[:], 0.0)
+        warm_out = keep.tile([P, 1], F32)
+        nc.scalar.activation(out=warm_out[:], in_=warm_in[:], func=ACT.Sigmoid)
+
+        z_sb, w_raw, c_sb, dh_sb = {}, {}, {}, {}
+
+        def load_z(s, g):
+            z_sb[s, g] = keep.tile([P, PACK, PASS], BF16, name="z_%d_%d" % (s, g))
+            rows = z[s * PASS:(s + 1) * PASS, g * PASS:(g + 1) * PASS]
+            nc.sync.dma_start(out=z_sb[s, g][:], in_=rows.rearrange("(p t) k -> p t k", t=PACK))
+
+        def load_w(g, half):
+            w_raw[g, half] = keep.tile([P, 2, GATES * H], U8, name="w_raw_%d_%d" % (g, half))
+            rows = w_bytes[g * PASS:(g + 1) * PASS, :].rearrange("(p t) n -> p t n", t=PACK)
+            nc.sync.dma_start(out=w_raw[g, half][:], in_=rows[:, 2 * half:2 * half + 2, :])
+
+        def load_tokens(tiles, name, src, s):
+            tiles[s] = keep.tile([P, PACK, H], BF16, name="%s_%d" % (name, s))
+            nc.sync.dma_start(out=tiles[s][:], in_=src[s * PASS:(s + 1) * PASS, :].rearrange("(p t) h -> p t h", t=PACK))
+
+        load_z(0, 0)
+        scale_sb = keep.tile([P, PASSES, PACK], F32)
+        nc.sync.dma_start(out=scale_sb[:], in_=w_scale.rearrange("(g p t) o -> p g (t o)", p=P, t=PACK))
+        a_sb = keep.tile([P, PASSES, PACK], BF16)
+        nc.sync.dma_start(out=a_sb[:], in_=a.rearrange("(g p t) -> p g t", p=P, t=PACK))
+        load_w(0, 0)
+        r_sb = keep.tile([P, PASSES, PACK], BF16)
+        nc.sync.dma_start(out=r_sb[:], in_=r.rearrange("(s p t) -> p s t", p=P, t=PACK))
+        load_w(0, 1)
+        load_z(0, 1)
+        load_w(1, 0)
+        load_w(1, 1)
+        nc.sync.dma_start(out=bias_rows[0:GATES * TILES, :], in_=b.rearrange("(x p) -> x p", p=P))
+        load_z(1, 0)
+        load_tokens(c_sb, "c", c, 0)
+        load_tokens(dh_sb, "dh", dh_new, 0)
+        load_z(1, 1)
+        load_tokens(c_sb, "c", c, 1)
+        load_tokens(dh_sb, "dh", dh_new, 1)
+
+        a_twice = keep.tile([P, PASSES, 2, PACK], BF16)
+        nc.gpsimd.tensor_copy(out=a_twice[:], in_=a_sb[:].unsqueeze(2).to_broadcast([P, PASSES, 2, PACK]))
+
+        w_wide, w_grouped, w_mx, w_bank = {}, {}, {}, {}
+
+        def widen_w(span, g, t):
+            first, count = WIDEN_SPANS[span]
+            if t == 0:
+                w_wide[span, g] = keep.tile([P, PACK, GATES, count * P], BF16, name="w_wide_%d_%d" % (span, g))
+            for gate in range(GATES):
+                col = gate * H + first * P
+                nc.scalar.activation(
+                    out=w_wide[span, g][:, t, gate, :], in_=w_raw[g, t // 2][:, t % 2, col:col + count * P].bitcast(FP8),
+                    func=ACT.Copy, scale=scale_sb[:, g, t:t + 1])
+
+        def wide_slice(j, g, gate):
+            span = min(j, len(WIDEN_SPANS) - 1)
+            col = (j - WIDEN_SPANS[span][0]) * P
+            return w_wide[span, g][:, :, gate, col:col + P]
+
+        def grouped_w(j):
+            if j not in w_grouped:
+                w_grouped[j] = work.tile([P, GATES, PASSES, P, PACK], BF16, name="w_grouped", align_bytes=64)
+                w_mx[j] = mx_tiles(keep, "w_%d" % j, GATES * PASSES * P)
+            return w_grouped[j]
+
+        def interleave_w_vector(j, g, gate):
+            nc.vector.tensor_copy(
+                out=grouped_w(j)[:, gate, g, :, :].rearrange("p (n i) t -> p n t i", i=4),
+                in_=wide_slice(j, g, gate).rearrange("p t (n i) -> p n t i", i=4))
+
+        def interleave_w_tensor(j, gate):
+            bank = spare_bank([P, PASSES, P, PACK], BF16)
+            for g in range(PASSES):
+                nc.tensor.matmul(out=bank[:, g, :, :].rearrange("p n t -> p t n"), lhsT=ident_bf16[:],
+                                 rhs=wide_slice(j, g, gate), start=True, stop=True)
+            w_bank[j, gate] = bank
+
+        def w_copy(j, gate):
+            nc.scalar.copy(out=grouped_w(j)[:, gate, :, :, :], in_=w_bank[j, gate][:])
+
+        def quantize_w(j, gate, count):
+            cols = slice(gate * PASSES * P, (gate + count) * PASSES * P)
+            quantize(w_mx[j][0][:, cols], w_mx[j][1][:, cols],
+                     w_grouped[j][:, gate:gate + count].rearrange("p x g n t -> p (x g n t)"))
+
+        za_grouped, za_mx, za_bank = {}, {}, {}
+
+        def za_transpose(s, g, u):
+            bank = spare_bank([P, 4, P], F32)
+            words = z_sb[s, g][:].bitcast(F32)
+            for e in range(2):
+                for v in range(2):
+                    nc.tensor.transpose(bank[:, 2 * e + v, :], words[:, 2 * u + e, v:PASS // 2:2], ident_f32[:])
+            za_bank[s, g, u] = bank
+
+        def za_scale(s, g, u):
+            if u == 0:
+                za_grouped[s, g] = work.tile([P, 2, P * 8], BF16, name="za_grouped", align_bytes=64)
+            gain = a_twice[:, g].rearrange("p e (v i) -> p (e v) i", i=2)
+            nc.vector.tensor_tensor(
+                out=za_grouped[s, g][:, u, :].rearrange("p (q x i) -> p q x i", x=4, i=2),
+                in0=za_bank[s, g, u][:].bitcast(BF16).rearrange("p x (q i) -> p q x i", i=2),
+                in1=gain.unsqueeze(1).to_broadcast([P, P, 4, 2]), op=ALU.mult)
+
+        def za_quantize(s, g):
+            za_mx[s, g] = mx_tiles(keep, "za_%d_%d" % (s, g), PASS)
+            quantize(za_mx[s, g][0][:], za_mx[s, g][1][:], za_grouped[s, g][:].rearrange("p u n -> p (u n)"))
+
+        zr_grouped, zr_mx, zr_bank = {}, {}, {}
+
+        def zr_interleave(s, g, half, borrow=None):
+            bank = spare_bank([P, 2, P, PACK], BF16, borrow)
+            for m in range(2):
+                col = (2 * half + m) * P
+                nc.tensor.matmul(out=bank[:, m, :, :].rearrange("p n t -> p t n"), lhsT=ident_bf16[:],
+                                 rhs=z_sb[s, g][:, :, col:col + P], start=True, stop=True)
+            zr_bank[s, g, half] = bank
+
+        def zr_scale(s, g, half):
+            if half == 0:
+                zr_grouped[s, g] = work.tile([P, 2, 2 * P, PACK], BF16, name="zr_grouped", align_bytes=64)
+            nc.vector.tensor_tensor(
+                out=zr_grouped[s, g][:, half], in0=zr_bank[s, g, half][:].rearrange("p m n t -> p (m n) t"),
+                in1=r_sb[:, s, :].unsqueeze(1).to_broadcast([P, 2 * P, PACK]), op=ALU.mult)
+
+        def zr_quantize(s, g):
+            zr_mx[s, g] = mx_tiles(keep, "zr_%d_%d" % (s, g), PASS)
+            quantize(zr_mx[s, g][0][:], zr_mx[s, g][1][:], zr_grouped[s, g][:].rearrange("p h n t -> p (h n t)"))
+
+        val = {}
+
+        def new(name, i, bufs=2):
+            val[name, i] = work.tile([P, PASS], F32, name=name, bufs=bufs)
+            return val[name, i][:]
+
+        def preact(i, gate):
+            j, s = divmod(i, PASSES)
+            bank = psum.tile([P, PASS], F32, name="p_bank_%d" % gate)
+            for g in range(PASSES):
+                col = (gate * PASSES + g) * P
+                matmul_mx(bank[:], w_mx[j], slice(col, col + P), za_mx[s, g], slice(0, PASS), g == 0, g == PASSES - 1)
+            val["p", gate, i] = bank
+
+        def gate_act(i, gate):
+            name, func, bufs = [("f", ACT.Sigmoid, 3), ("g", ACT.Tanh, 3), ("o", ACT.Sigmoid, 3)][gate]
+            col = gate * TILES + i // PASSES
+            nc.scalar.activation(out=new(name, i, bufs), in_=val["p", gate, i][:], func=func, bias=bias_sb[:, col:col + 1])
+
+        def act(name, func, src, i, bufs=2):
+            nc.scalar.activation(out=new(name, i, bufs), in_=val[src, i][:], func=func)
+
+        def cd_transpose(i):
+            j, s = divmod(i, PASSES)
+            bank = psum.tile([P, 2, PACK, P], BF16, name="cd_bank")
+            for x, src in enumerate((c_sb, dh_sb)):
+                for t in range(PACK):
+                    nc.tensor.transpose(bank[:, x, t, :], src[s][:, t, j * P:(j + 1) * P], ident_bf16[:])
+            val["cd", i] = bank
+
+        def tt(name, x, y, op, i):
+            nc.vector.tensor_tensor(out=new(name, i), in0=val[x, i][:], in1=val[y, i][:], op=op)
+
+        def stt(dst, x, scalar, op0, y, i):
+            nc.vector.scalar_tensor_tensor(out=dst, in0=val[x, i][:], scalar=scalar, in1=val[y, i][:], op0=op0, op1=ALU.mult)
+
+        def op_d(i):
+            nc.vector.tensor_tensor(
+                out=new("d", i).rearrange("p (u q e) -> p u q e", u=2, e=2),
+                in0=val["cd", i][:, 0].rearrange("p (u e) q -> p u q e", e=2),
+                in1=val["g", i][:].rearrange("p (u q e) -> p u q e", u=2, e=2), op=ALU.subtract)
+
+        def op_na(i):
+            dst = new("na", i).rearrange("p (u q e) -> p u q e", u=2, e=2)
+            for u in range(2):
+                nc.vector.scalar_tensor_tensor(
+                    out=dst[:, u], in0=val["cd", i][:, 1, 2 * u:2 * u + 2, :].rearrange("p e q -> p q e"), scalar=-1.0,
+                    in1=val["o", i][:].rearrange("p (u q e) -> p u q e", u=2, e=2)[:, u], op0=ALU.mult, op1=ALU.mult)
+
+        def new_delta(gate, i):
+            val["delta", gate, i] = work.tile([P, PASS], BF16, name="delta_%d" % gate)
+            return val["delta", gate, i][:]
+
+        def delta_transpose(i, gates, borrow=None):
+            bank = psum.tile([P, len(gates), 2, P], F32, name=borrow or "delta_bank_%d" % gates[0])
+            for x, gate in enumerate(gates):
+                words = val["delta", gate, i][:].bitcast(F32)
+                for u in range(2):
+                    nc.tensor.transpose(bank[:, x, u, :], words[:, u * P:(u + 1) * P], ident_f32[:])
+            val["dbank", gates[0], i] = bank
+
+        def delta_copy(i, gates):
+            grouped = work.tile([P, len(gates) * PASS], BF16, name="delta_grouped_%d" % gates[0], align_bytes=64)
+            nc.scalar.copy(out=grouped[:].bitcast(F32).rearrange("p (x h u) -> p x h u", h=P, u=2),
+                           in_=val["dbank", gates[0], i][:].rearrange("p x u h -> p x h u"))
+            val["dgrouped", gates[0], i] = grouped
+
+        def delta_quantize(i, gates):
+            tiles = mx_tiles(work, "delta_%d" % gates[0], len(gates) * P, bufs=4)
+            quantize(tiles[0][:], tiles[1][:], val["dgrouped", gates[0], i][:])
+            for x, gate in enumerate(gates):
+                val["dmx", gate, i] = (tiles, slice(x * P, (x + 1) * P))
+
+        def out_matmul(j, gate, g, borrow=None):
+            bank = spare_bank([P, 4, P], F32, borrow)
+            for m in range(4):
+                for s in range(PASSES):
+                    tiles, cols = val["dmx", gate, j * PASSES + s]
+                    matmul_mx(bank[:, m, :], zr_mx[s, g], slice(m * P, (m + 1) * P), tiles, cols, s == 0, s == PASSES - 1)
+            val["obank", j, gate, g] = bank
+
+        def out_store(j, gate, g, on_vector=False):
+            stage = work.tile([P, 4, P], F32, name="stage", bufs=6)
+            if on_vector:
+                nc.vector.tensor_copy(out=stage[:], in_=val["obank", j, gate, g][:])
+            else:
+                nc.scalar.copy(out=stage[:], in_=val["obank", j, gate, g][:])
+            col = gate * H + j * P
+            nc.sync.dma_start(out=out[g * PASS:(g + 1) * PASS, col:col + P].rearrange("(m p) n -> p m n", p=P), in_=stage[:])
+
+        FG, O = (GATE_F, GATE_G), (GATE_O,)
+
+        za_transpose(0, 0, 0)
+        za_transpose(0, 0, 1)
+        for t in range(PACK):
+            widen_w(0, 0, t)
+        zr_interleave(0, 0, 0, "delta_bank_0")
+        zr_interleave(0, 0, 1, "delta_bank_2")
+        za_scale(0, 0, 0)
+        za_scale(0, 0, 1)
+        za_transpose(0, 1, 0)
+        za_transpose(0, 1, 1)
+        zr_scale(0, 0, 0)
+        za_quantize(0, 0)
+        zr_scale(0, 0, 1)
+        zr_interleave(0, 1, 0, "delta_bank_0")
+        zr_interleave(0, 1, 1, "delta_bank_2")
+        for gate in range(GATES):
+            interleave_w_vector(0, 0, gate)
+        for t in range(PACK):
+            widen_w(0, 1, t)
+        za_scale(0, 1, 0)
+        za_scale(0, 1, 1)
+        bias_bank = psum.tile([P, P], BF16, name="cd_bank")
+        nc.tensor.transpose(bias_bank[:], bias_rows[:], ident_bf16[:])
+        za_transpose(1, 0, 0)
+        za_transpose(1, 0, 1)
+        interleave_w_vector(0, 1, 0)
+        za_quantize(0, 1)
+        interleave_w_vector(0, 1, 1)
+        quantize_w(0, 0, 1)
+        preact(0, 0)
+        bias_sb = keep.tile([P, GATES * TILES], F32)
+        nc.vector.tensor_copy(out=bias_sb[:], in_=bias_bank[:, 0:GATES * TILES])
+        interleave_w_vector(0, 1, 2)
+        quantize_w(0, 1, 1)
+        preact(0, 1)
+        za_scale(1, 0, 0)
+        quantize_w(0, 2, 1)
+        preact(0, 2)
+        cd_transpose(0)
+        for g in range(PASSES):
+            for t in range(PACK):
+                widen_w(1, g, t)
+        za_scale(1, 0, 1)
+        za_transpose(1, 1, 0)
+        za_transpose(1, 1, 1)
+        zr_quantize(0, 0)
+        zr_scale(0, 1, 0)
+        za_quantize(1, 0)
+        zr_scale(0, 1, 1)
+        gate_act(0, GATE_F)
+        gate_act(0, GATE_G)
+        gate_act(0, GATE_O)
+        act("g2", ACT.Square, "g", 0, 3)
+
+        za_scale(1, 1, 0)
+        za_scale(1, 1, 1)
+        interleave_w_tensor(1, 0)
+        interleave_w_tensor(1, 1)
+        op_d(0)
+        za_quantize(1, 1)
+        for gate in (GATE_G, GATE_F, GATE_O):
+            preact(1, gate)
+        widen_w(2, 0, 0)
+        widen_w(2, 0, 1)
+        w_copy(1, 0)
+        w_copy(1, 1)
+        interleave_w_tensor(1, 2)
+        zr_interleave(1, 0, 0, "delta_bank_0")
+        widen_w(2, 0, 2)
+        tt("fd", "f", "d", ALU.mult, 0)
+        op_na(0)
+        tt("cn", "fd", "g", ALU.add, 0)
+        cd_transpose(1)
+        zr_interleave(1, 0, 1, "delta_bank_2")
+        gate_act(1, GATE_G)
+        gate_act(1, GATE_F)
+        act("tc", ACT.Tanh, "cn", 0)
+        w_copy(1, 2)
+        act("s", ACT.Square, "tc", 0)
+        gate_act(1, GATE_O)
+        act("g2", ACT.Square, "g", 1, 3)
+        widen_w(2, 0, 3)
+        zr_quantize(0, 1)
+        quantize_w(1, 0, 2)
+        zr_scale(1, 0, 0)
+        quantize_w(1, 2, 1)
+        zr_scale(1, 0, 1)
+
+        def zr_job(s, g, half):
+            return (lambda: zr_interleave(s, g, half), lambda: zr_scale(s, g, half))
+
+        def w_job(j, gate):
+            return (lambda: interleave_w_tensor(j, gate), lambda: w_copy(j, gate))
+
+        def out_job(j, gate, g, on_vector=False):
+            return (lambda: out_matmul(j, gate, g), lambda: out_store(j, gate, g, on_vector))
+
+        def out_jobs(j):
+            return [out_job(j, gate, g) for gate in (GATE_O, GATE_F, GATE_G) for g in range(PASSES)]
+
+        idle = (lambda: None, lambda: None)
+        jobs = {
+            1: [zr_job(1, 1, 0), zr_job(1, 1, 1), idle, w_job(2, 0)],
+            2: [w_job(2, 1), w_job(2, 2), w_job(3, 0), w_job(3, 1)],
+            3: out_jobs(0)[:2] + [w_job(3, 2), out_jobs(0)[2]],
+            4: out_jobs(0)[3:] + [idle],
+            5: out_jobs(1)[:3] + [idle],
+            6: out_jobs(1)[3:] + [idle],
+            7: out_jobs(2)[:4],
+        }
+
+        for i in range(1, UNITS):
+            nxt, old = i + 1 < UNITS, i >= 2
+            if old:
+                delta_copy(i - 2, FG)
+            if nxt:
+                for gate in (GATE_G, GATE_F, GATE_O):
+                    preact(i + 1, gate)
+            stt(new("dct", i - 1), "s", 1.0, ALU.subtract, "na", i - 1)
+            if old:
+                delta_quantize(i - 2, O)
+            else:
+                zr_quantize(1, 0)
+            jobs[i][0][0]()
+            jobs[i][1][0]()
+            if i == 1:
+                for t in range(2):
+                    widen_w(2, 1, t)
+            op_d(i)
+            stt(new("nq", i - 1), "f", 1.0, ALU.subtract, "dct", i - 1)
+            tt("fd", "f", "d", ALU.mult, i)
+            if old:
+                delta_quantize(i - 2, FG)
+            tt("nm", "na", "tc", ALU.mult, i - 1)
+            if nxt:
+                gate_act(i + 1, GATE_G)
+                gate_act(i + 1, GATE_F)
+            jobs[i][0][1]()
+            tt("cn", "fd", "g", ALU.add, i)
+            jobs[i][1][1]()
+            jobs[i][2][0]()
+            if not nxt:
+                out_matmul(2, GATE_G, 0, "p_bank_0")
+                out_matmul(2, GATE_G, 1, "p_bank_1")
+            act("tc", ACT.Tanh, "cn", i)
+            if nxt:
+                gate_act(i + 1, GATE_O)
+            else:
+                jobs[i][2][1]()
+            act("s", ACT.Square, "tc", i)
+            if i == 1:
+                for t in range(2, PACK):
+                    widen_w(2, 1, t)
+            stt(new_delta(GATE_O, i - 1), "o", 1.0, ALU.subtract, "nm", i - 1)
+            delta_transpose(i - 1, O)
+            op_na(i)
+            if nxt:
+                cd_transpose(i + 1)
+                act("g2", ACT.Square, "g", i + 1, 3)
+            jobs[i][3][0]()
+            delta_copy(i - 1, O)
+            stt(new_delta(GATE_F, i - 1), "nq", -1.0, ALU.mult, "fd", i - 1)
+            if nxt:
+                jobs[i][2][1]()
+            stt(new_delta(GATE_G, i - 1), "g2", 1.0, ALU.subtract, "nq", i - 1)
+            delta_transpose(i - 1, FG)
+            jobs[i][3][1]()
+            if i == 1:
+                zr_quantize(1, 1)
+            if i in (2, 4):
+                quantize_w(i // 2 + 1, 0, 2)
+                quantize_w(i // 2 + 1, 2, 1)
+
+        last, j = UNITS - 1, TILES - 1
+        delta_copy(last - 1, FG)
+        out_store(2, GATE_G, 0)
+        out_store(2, GATE_G, 1)
+        tt("nm", "na", "tc", ALU.mult, last)
+        delta_quantize(last - 1, O)
+        stt(new("dct", last), "s", 1.0, ALU.subtract, "na", last)
+        stt(new_delta(GATE_O, last), "o", 1.0, ALU.subtract, "nm", last)
+        delta_transpose(last, O)
+        delta_copy(last, O)
+        stt(new("nq", last), "f", 1.0, ALU.subtract, "dct", last)
+        delta_quantize(last - 1, FG)
+        stt(new_delta(GATE_F, last), "nq", -1.0, ALU.mult, "fd", last)
+        delta_transpose(last, (GATE_F,))
+        delta_copy(last, (GATE_F,))
+        delta_quantize(last, O)
+        out_matmul(j, GATE_O, 0, "p_bank_2")
+        stt(new_delta(GATE_G, last), "g2", 1.0, ALU.subtract, "nq", last)
+        delta_transpose(last, (GATE_G,), "cd_bank")
+        out_matmul(j, GATE_O, 1)
+        delta_quantize(last, (GATE_F,))
+        out_store(j, GATE_O, 0)
+        delta_copy(last, (GATE_G,))
+        out_matmul(j, GATE_F, 0)
+        out_matmul(j, GATE_F, 1, "p_bank_0")
+        out_store(j, GATE_O, 1, True)
+        delta_quantize(last, (GATE_G,))
+        out_matmul(j, GATE_G, 0, "p_bank_1")
+        out_matmul(j, GATE_G, 1, "delta_bank_2")
+        for gate in FG:
+            out_store(j, gate, 0)
+            out_store(j, gate, 1, True)

@@ -32,7 +32,7 @@ def tile_coupledlstmfoldedweightgradient_kernel(tc, z, c, w_bytes, w_scale, b, a
         keep = ctx.enter_context(tc.tile_pool(name="keep", bufs=1))
         work = ctx.enter_context(tc.tile_pool(name="work", bufs=2))
         psum = ctx.enter_context(tc.psum_pool(name="psum", bufs=1))
-        ctx.enter_context(tc.manual_schedule())
+        ctx.enter_context(tc.manual_schedule(engines={mybir.EngineType.SP}))
 
         def quantize(codes, scales, values):
             nc.vector.quantize_mx(out=codes.bitcast(FP8X4), scales=scales, in_=values)
@@ -65,10 +65,13 @@ def tile_coupledlstmfoldedweightgradient_kernel(tc, z, c, w_bytes, w_scale, b, a
 
         z_sb, w_raw, c_sb, dh_sb = {}, {}, {}, {}
 
-        def load_z(s, g):
+        def load_z(s, g, parts=1):
             z_sb[s, g] = keep.tile([P, PACK, PASS], BF16, name="z_%d_%d" % (s, g))
             rows = z[s * PASS:(s + 1) * PASS, g * PASS:(g + 1) * PASS]
-            nc.sync.dma_start(out=z_sb[s, g][:], in_=rows.rearrange("(p t) k -> p t k", t=PACK))
+            words = rows.rearrange("(p t) k -> p t k", t=PACK).bitcast(F32)
+            for part in range(parts):
+                span = slice(part * PACK // parts, (part + 1) * PACK // parts)
+                nc.sync.dma_start(out=z_sb[s, g][:].bitcast(F32)[:, span, :], in_=words[:, span, :])
 
         def load_w(g, half):
             w_raw[g, half] = keep.tile([P, 2, GATES * H], U8, name="w_raw_%d_%d" % (g, half))
@@ -79,11 +82,11 @@ def tile_coupledlstmfoldedweightgradient_kernel(tc, z, c, w_bytes, w_scale, b, a
             tiles[s] = keep.tile([P, PACK, H], BF16, name="%s_%d" % (name, s))
             nc.sync.dma_start(out=tiles[s][:], in_=src[s * PASS:(s + 1) * PASS, :].rearrange("(p t) h -> p t h", t=PACK))
 
-        load_z(0, 0)
-        scale_sb = keep.tile([P, PASSES, PACK], F32)
-        nc.sync.dma_start(out=scale_sb[:], in_=w_scale.rearrange("(g p t) o -> p g (t o)", p=P, t=PACK))
         a_sb = keep.tile([P, PASSES, PACK], BF16)
         nc.sync.dma_start(out=a_sb[:], in_=a.rearrange("(g p t) -> p g t", p=P, t=PACK))
+        load_z(0, 0, 2)
+        scale_sb = keep.tile([P, PASSES, PACK], F32)
+        nc.sync.dma_start(out=scale_sb[:], in_=w_scale.rearrange("(g p t) o -> p g (t o)", p=P, t=PACK))
         load_w(0, 0)
         r_sb = keep.tile([P, PASSES, PACK], BF16)
         nc.sync.dma_start(out=r_sb[:], in_=r.rearrange("(s p t) -> p s t", p=P, t=PACK))
@@ -204,7 +207,7 @@ def tile_coupledlstmfoldedweightgradient_kernel(tc, z, c, w_bytes, w_scale, b, a
             val["p", gate, i] = bank
 
         def gate_act(i, gate):
-            name, func, bufs = [("f", ACT.Sigmoid, 3), ("g", ACT.Tanh, 3), ("o", ACT.Sigmoid, 3)][gate]
+            name, func, bufs = [("f", ACT.Sigmoid, 3), ("g", ACT.Tanh, 2), ("o", ACT.Sigmoid, 3)][gate]
             col = gate * TILES + i // PASSES
             nc.scalar.activation(out=new(name, i, bufs), in_=val["p", gate, i][:], func=func, bias=bias_sb[:, col:col + 1])
 
@@ -242,42 +245,47 @@ def tile_coupledlstmfoldedweightgradient_kernel(tc, z, c, w_bytes, w_scale, b, a
             val["delta", gate, i] = work.tile([P, PASS], BF16, name="delta_%d" % gate)
             return val["delta", gate, i][:]
 
-        def delta_transpose(i, gates, borrow=None):
-            bank = psum.tile([P, len(gates), 2, P], F32, name=borrow or "delta_bank_%d" % gates[0])
-            for x, gate in enumerate(gates):
-                words = val["delta", gate, i][:].bitcast(F32)
+        def delta_transpose(items, bank_name):
+            bank = psum.tile([P, len(items), 2, P], F32, name=bank_name)
+            for x, item in enumerate(items):
+                words = val[("delta",) + item][:].bitcast(F32)
                 for u in range(2):
                     nc.tensor.transpose(bank[:, x, u, :], words[:, u * P:(u + 1) * P], ident_f32[:])
-            val["dbank", gates[0], i] = bank
+            val["dbank", items] = bank
 
-        def delta_copy(i, gates):
-            grouped = work.tile([P, len(gates) * PASS], BF16, name="delta_grouped_%d" % gates[0], align_bytes=64)
+        def delta_copy(items):
+            grouped = work.tile([P, len(items) * PASS], BF16, name="delta_grouped_%d" % len(items), bufs=3, align_bytes=64)
             nc.scalar.copy(out=grouped[:].bitcast(F32).rearrange("p (x h u) -> p x h u", h=P, u=2),
-                           in_=val["dbank", gates[0], i][:].rearrange("p x u h -> p x h u"))
-            val["dgrouped", gates[0], i] = grouped
+                           in_=val["dbank", items][:].rearrange("p x u h -> p x h u"))
+            val["dgrouped", items] = grouped
 
-        def delta_quantize(i, gates):
-            tiles = mx_tiles(work, "delta_%d" % gates[0], len(gates) * P, bufs=4)
-            quantize(tiles[0][:], tiles[1][:], val["dgrouped", gates[0], i][:])
-            for x, gate in enumerate(gates):
-                val["dmx", gate, i] = (tiles, slice(x * P, (x + 1) * P))
+        def delta_quantize(items):
+            tiles = mx_tiles(work, "delta_%d" % len(items), len(items) * P, bufs=5)
+            quantize(tiles[0][:], tiles[1][:], val["dgrouped", items][:])
+            for x, item in enumerate(items):
+                val[("dmx",) + item] = (tiles, slice(x * P, (x + 1) * P))
 
-        def out_matmul(j, gate, g, borrow=None):
-            bank = spare_bank([P, 4, P], F32, borrow)
-            for m in range(4):
+        def fg(i):
+            return ((GATE_F, i), (GATE_G, i))
+
+        def one(gate, i):
+            return ((gate, i),)
+
+        def out_matmul(j, gate, g, borrow=None, first=0, count=4):
+            bank = spare_bank([P, count, P], F32, borrow)
+            for x in range(count):
+                m = first + x
                 for s in range(PASSES):
                     tiles, cols = val["dmx", gate, j * PASSES + s]
-                    matmul_mx(bank[:, m, :], zr_mx[s, g], slice(m * P, (m + 1) * P), tiles, cols, s == 0, s == PASSES - 1)
-            val["obank", j, gate, g] = bank
+                    matmul_mx(bank[:, x, :], zr_mx[s, g], slice(m * P, (m + 1) * P), tiles, cols, s == 0, s == PASSES - 1)
+            val["obank", j, gate, g, first] = bank
 
-        def out_store(j, gate, g, on_vector=False):
-            stage = work.tile([P, 4, P], F32, name="stage", bufs=6)
-            if on_vector:
-                nc.vector.tensor_copy(out=stage[:], in_=val["obank", j, gate, g][:])
-            else:
-                nc.scalar.copy(out=stage[:], in_=val["obank", j, gate, g][:])
-            col = gate * H + j * P
-            nc.sync.dma_start(out=out[g * PASS:(g + 1) * PASS, col:col + P].rearrange("(m p) n -> p m n", p=P), in_=stage[:])
+        def out_store(j, gate, g, on_vector=False, first=0, count=4):
+            stage = work.tile([P, count, P], F32, name="stage_%d" % count, bufs=4 if count == 4 else 8)
+            copy = nc.vector.tensor_copy if on_vector else nc.scalar.copy
+            copy(out=stage[:], in_=val["obank", j, gate, g, first][:])
+            row, col = g * PASS + first * P, gate * H + j * P
+            nc.sync.dma_start(out=out[row:row + count * P, col:col + P].rearrange("(m p) n -> p m n", p=P), in_=stage[:])
 
         FG, O = (GATE_F, GATE_G), (GATE_O,)
 
@@ -347,14 +355,14 @@ def tile_coupledlstmfoldedweightgradient_kernel(tc, z, c, w_bytes, w_scale, b, a
         widen_w(2, 0, 1)
         w_copy(1, 0)
         w_copy(1, 1)
-        interleave_w_tensor(1, 2)
         zr_interleave(1, 0, 0, "delta_bank_0")
+        interleave_w_tensor(1, 2)
         widen_w(2, 0, 2)
         tt("fd", "f", "d", ALU.mult, 0)
         op_na(0)
         tt("cn", "fd", "g", ALU.add, 0)
-        cd_transpose(1)
         zr_interleave(1, 0, 1, "delta_bank_2")
+        cd_transpose(1)
         gate_act(1, GATE_G)
         gate_act(1, GATE_F)
         act("tc", ACT.Tanh, "cn", 0)
@@ -389,64 +397,53 @@ def tile_coupledlstmfoldedweightgradient_kernel(tc, z, c, w_bytes, w_scale, b, a
             4: out_jobs(0)[3:] + [idle],
             5: out_jobs(1)[:3] + [idle],
             6: out_jobs(1)[3:] + [idle],
-            7: out_jobs(2)[:4],
         }
 
-        for i in range(1, UNITS):
-            nxt, old = i + 1 < UNITS, i >= 2
+        for i in range(1, UNITS - 1):
+            old = i >= 2
             if old:
-                delta_copy(i - 2, FG)
-            if nxt:
-                for gate in (GATE_G, GATE_F, GATE_O):
-                    preact(i + 1, gate)
+                delta_copy(fg(i - 2))
+            for gate in (GATE_G, GATE_F, GATE_O):
+                preact(i + 1, gate)
             stt(new("dct", i - 1), "s", 1.0, ALU.subtract, "na", i - 1)
-            if old:
-                delta_quantize(i - 2, O)
-            else:
-                zr_quantize(1, 0)
-            jobs[i][0][0]()
-            jobs[i][1][0]()
             if i == 1:
                 for t in range(2):
                     widen_w(2, 1, t)
             op_d(i)
+            if old:
+                delta_quantize(one(GATE_O, i - 2))
+            else:
+                zr_quantize(1, 0)
+            jobs[i][0][0]()
+            jobs[i][1][0]()
             stt(new("nq", i - 1), "f", 1.0, ALU.subtract, "dct", i - 1)
             tt("fd", "f", "d", ALU.mult, i)
             if old:
-                delta_quantize(i - 2, FG)
+                delta_quantize(fg(i - 2))
             tt("nm", "na", "tc", ALU.mult, i - 1)
-            if nxt:
-                gate_act(i + 1, GATE_G)
-                gate_act(i + 1, GATE_F)
+            gate_act(i + 1, GATE_G)
+            gate_act(i + 1, GATE_F)
             jobs[i][0][1]()
             tt("cn", "fd", "g", ALU.add, i)
             jobs[i][1][1]()
             jobs[i][2][0]()
-            if not nxt:
-                out_matmul(2, GATE_G, 0, "p_bank_0")
-                out_matmul(2, GATE_G, 1, "p_bank_1")
             act("tc", ACT.Tanh, "cn", i)
-            if nxt:
-                gate_act(i + 1, GATE_O)
-            else:
-                jobs[i][2][1]()
+            gate_act(i + 1, GATE_O)
             act("s", ACT.Square, "tc", i)
+            stt(new_delta(GATE_O, i - 1), "o", 1.0, ALU.subtract, "nm", i - 1)
+            delta_transpose(one(GATE_O, i - 1), "delta_bank_2")
+            op_na(i)
+            cd_transpose(i + 1)
+            act("g2", ACT.Square, "g", i + 1, 3)
+            delta_copy(one(GATE_O, i - 1))
             if i == 1:
                 for t in range(2, PACK):
                     widen_w(2, 1, t)
-            stt(new_delta(GATE_O, i - 1), "o", 1.0, ALU.subtract, "nm", i - 1)
-            delta_transpose(i - 1, O)
-            op_na(i)
-            if nxt:
-                cd_transpose(i + 1)
-                act("g2", ACT.Square, "g", i + 1, 3)
             jobs[i][3][0]()
-            delta_copy(i - 1, O)
             stt(new_delta(GATE_F, i - 1), "nq", -1.0, ALU.mult, "fd", i - 1)
-            if nxt:
-                jobs[i][2][1]()
+            jobs[i][2][1]()
             stt(new_delta(GATE_G, i - 1), "g2", 1.0, ALU.subtract, "nq", i - 1)
-            delta_transpose(i - 1, FG)
+            delta_transpose(fg(i - 1), "delta_bank_0")
             jobs[i][3][1]()
             if i == 1:
                 zr_quantize(1, 1)
@@ -454,35 +451,72 @@ def tile_coupledlstmfoldedweightgradient_kernel(tc, z, c, w_bytes, w_scale, b, a
                 quantize_w(i // 2 + 1, 0, 2)
                 quantize_w(i // 2 + 1, 2, 1)
 
-        last, j = UNITS - 1, TILES - 1
-        delta_copy(last - 1, FG)
-        out_store(2, GATE_G, 0)
-        out_store(2, GATE_G, 1)
+        last, prev, j = UNITS - 1, UNITS - 2, TILES - 1
+
+        def finish(gate, i, bank_name):
+            if gate == GATE_F:
+                stt(new_delta(gate, i), "nq", -1.0, ALU.mult, "fd", i)
+            elif gate == GATE_G:
+                stt(new_delta(gate, i), "g2", 1.0, ALU.subtract, "nq", i)
+            else:
+                stt(new_delta(gate, i), "o", 1.0, ALU.subtract, "nm", i)
+            delta_transpose(one(gate, i), bank_name)
+
+        delta_copy(fg(prev - 1))
+        op_d(last)
+        delta_quantize(one(GATE_O, prev - 1))
+        out_matmul(j - 1, GATE_O, 0)
+        out_matmul(j - 1, GATE_O, 1)
+        tt("nm", "na", "tc", ALU.mult, prev)
+        tt("fd", "f", "d", ALU.mult, last)
+        delta_quantize(fg(prev - 1))
+        out_matmul(j - 1, GATE_F, 0, "p_bank_0")
+        out_matmul(j - 1, GATE_F, 1, "p_bank_1")
+        out_store(j - 1, GATE_O, 0)
+        out_store(j - 1, GATE_O, 1)
+        finish(GATE_O, prev, "delta_bank_2")
+        out_matmul(j - 1, GATE_G, 0, "p_bank_2")
+        out_matmul(j - 1, GATE_G, 1)
+        tt("cn", "fd", "g", ALU.add, last)
+        out_store(j - 1, GATE_F, 0)
+        act("tc", ACT.Tanh, "cn", last)
+        delta_copy(one(GATE_O, prev))
+        act("s", ACT.Square, "tc", last)
+        out_store(j - 1, GATE_F, 1)
+        out_store(j - 1, GATE_G, 0)
+        stt(new("dct", prev), "s", 1.0, ALU.subtract, "na", prev)
+        op_na(last)
+        stt(new("nq", prev), "f", 1.0, ALU.subtract, "dct", prev)
         tt("nm", "na", "tc", ALU.mult, last)
-        delta_quantize(last - 1, O)
+        delta_quantize(one(GATE_O, prev))
+        finish(GATE_O, last, "delta_bank_2")
+        delta_copy(one(GATE_O, last))
+        out_store(j - 1, GATE_G, 1)
         stt(new("dct", last), "s", 1.0, ALU.subtract, "na", last)
-        stt(new_delta(GATE_O, last), "o", 1.0, ALU.subtract, "nm", last)
-        delta_transpose(last, O)
-        delta_copy(last, O)
+        finish(GATE_F, prev, "delta_bank_0")
+        delta_copy(one(GATE_F, prev))
+        delta_quantize(one(GATE_O, last))
+        out_matmul(j, GATE_O, 0, "p_bank_0")
+        out_matmul(j, GATE_O, 1, "p_bank_1")
         stt(new("nq", last), "f", 1.0, ALU.subtract, "dct", last)
-        delta_quantize(last - 1, FG)
-        stt(new_delta(GATE_F, last), "nq", -1.0, ALU.mult, "fd", last)
-        delta_transpose(last, (GATE_F,))
-        delta_copy(last, (GATE_F,))
-        delta_quantize(last, O)
-        out_matmul(j, GATE_O, 0, "p_bank_2")
-        stt(new_delta(GATE_G, last), "g2", 1.0, ALU.subtract, "nq", last)
-        delta_transpose(last, (GATE_G,), "cd_bank")
-        out_matmul(j, GATE_O, 1)
-        delta_quantize(last, (GATE_F,))
+        delta_quantize(one(GATE_F, prev))
+        finish(GATE_F, last, "delta_bank_0")
         out_store(j, GATE_O, 0)
-        delta_copy(last, (GATE_G,))
-        out_matmul(j, GATE_F, 0)
-        out_matmul(j, GATE_F, 1, "p_bank_0")
-        out_store(j, GATE_O, 1, True)
-        delta_quantize(last, (GATE_G,))
-        out_matmul(j, GATE_G, 0, "p_bank_1")
-        out_matmul(j, GATE_G, 1, "delta_bank_2")
-        for gate in FG:
-            out_store(j, gate, 0)
-            out_store(j, gate, 1, True)
+        out_store(j, GATE_O, 1)
+        delta_copy(one(GATE_F, last))
+        finish(GATE_G, prev, "cd_bank")
+        delta_copy(one(GATE_G, prev))
+        finish(GATE_G, last, "delta_bank_2")
+        delta_quantize(one(GATE_F, last))
+        delta_copy(one(GATE_G, last))
+        delta_quantize(one(GATE_G, prev))
+        halves = [(g, first) for g in range(PASSES) for first in (0, 2)]
+        for (g, first), bank_name in zip(halves, (None, None, "p_bank_2", "p_bank_0")):
+            out_matmul(j, GATE_F, g, bank_name, first, 2)
+        delta_quantize(one(GATE_G, last))
+        for x, (g, first) in enumerate(halves):
+            out_store(j, GATE_F, g, x % 2 == 1, first, 2)
+        for (g, first), bank_name in zip(halves, ("p_bank_1", "cd_bank", "delta_bank_0", "delta_bank_2")):
+            out_matmul(j, GATE_G, g, bank_name, first, 2)
+        for x, (g, first) in enumerate(halves):
+            out_store(j, GATE_G, g, x % 2 == 1, first, 2)

@@ -32,7 +32,7 @@ def tile_coupledlstmfoldedweightgradient_kernel(tc, z, c, w_bytes, w_scale, b, a
         keep = ctx.enter_context(tc.tile_pool(name="keep", bufs=1))
         work = ctx.enter_context(tc.tile_pool(name="work", bufs=2))
         psum = ctx.enter_context(tc.psum_pool(name="psum", bufs=1))
-        ctx.enter_context(tc.manual_schedule(engines={mybir.EngineType.SP}))
+        ctx.enter_context(tc.manual_schedule())
 
         def quantize(codes, scales, values):
             nc.vector.quantize_mx(out=codes.bitcast(FP8X4), scales=scales, in_=values)
@@ -90,8 +90,8 @@ def tile_coupledlstmfoldedweightgradient_kernel(tc, z, c, w_bytes, w_scale, b, a
         load_w(0, 0)
         r_sb = keep.tile([P, PASSES, PACK], BF16)
         nc.sync.dma_start(out=r_sb[:], in_=r.rearrange("(s p t) -> p s t", p=P, t=PACK))
-        load_w(0, 1)
         load_z(0, 1)
+        load_w(0, 1)
         load_w(1, 0)
         load_w(1, 1)
         nc.sync.dma_start(out=bias_rows[0:GATES * TILES, :], in_=b.rearrange("(x p) -> x p", p=P))
@@ -107,15 +107,18 @@ def tile_coupledlstmfoldedweightgradient_kernel(tc, z, c, w_bytes, w_scale, b, a
 
         w_wide, w_grouped, w_mx, w_bank = {}, {}, {}, {}
 
-        def widen_w(span, g, t):
+        def widen_w(span, g, t, on_vector=False):
             first, count = WIDEN_SPANS[span]
             if t == 0:
                 w_wide[span, g] = keep.tile([P, PACK, GATES, count * P], BF16, name="w_wide_%d_%d" % (span, g))
             for gate in range(GATES):
                 col = gate * H + first * P
-                nc.scalar.activation(
-                    out=w_wide[span, g][:, t, gate, :], in_=w_raw[g, t // 2][:, t % 2, col:col + count * P].bitcast(FP8),
-                    func=ACT.Copy, scale=scale_sb[:, g, t:t + 1])
+                dst = w_wide[span, g][:, t, gate, :]
+                src = w_raw[g, t // 2][:, t % 2, col:col + count * P].bitcast(FP8)
+                if on_vector:
+                    nc.vector.tensor_scalar(out=dst, in0=src, scalar1=scale_sb[:, g, t:t + 1], scalar2=None, op0=ALU.mult)
+                else:
+                    nc.scalar.activation(out=dst, in_=src, func=ACT.Copy, scale=scale_sb[:, g, t:t + 1])
 
         def wide_slice(j, g, gate):
             span = min(j, len(WIDEN_SPANS) - 1)
@@ -139,6 +142,16 @@ def tile_coupledlstmfoldedweightgradient_kernel(tc, z, c, w_bytes, w_scale, b, a
                 nc.tensor.matmul(out=bank[:, g, :, :].rearrange("p n t -> p t n"), lhsT=ident_bf16[:],
                                  rhs=wide_slice(j, g, gate), start=True, stop=True)
             w_bank[j, gate] = bank
+
+        def first_w_tensor(gates, borrow):
+            bank = spare_bank([P, len(gates), P, PACK], BF16, borrow)
+            for x, gate in enumerate(gates):
+                nc.tensor.matmul(out=bank[:, x, :, :].rearrange("p n t -> p t n"), lhsT=ident_bf16[:],
+                                 rhs=wide_slice(0, 0, gate), start=True, stop=True)
+            w_bank[0, gates] = bank
+
+        def first_w_copy(gates):
+            nc.scalar.copy(out=grouped_w(0)[:, gates[0]:gates[-1] + 1, 0, :, :], in_=w_bank[0, gates][:])
 
         def w_copy(j, gate):
             nc.scalar.copy(out=grouped_w(j)[:, gate, :, :, :], in_=w_bank[j, gate][:])
@@ -289,10 +302,18 @@ def tile_coupledlstmfoldedweightgradient_kernel(tc, z, c, w_bytes, w_scale, b, a
 
         FG, O = (GATE_F, GATE_G), (GATE_O,)
 
+        def finish(gate, i, bank_name):
+            if gate == GATE_F:
+                stt(new_delta(gate, i), "nq", -1.0, ALU.mult, "fd", i)
+            elif gate == GATE_G:
+                stt(new_delta(gate, i), "g2", 1.0, ALU.subtract, "nq", i)
+            else:
+                stt(new_delta(gate, i), "o", 1.0, ALU.subtract, "nm", i)
+            if bank_name:
+                delta_transpose(one(gate, i), bank_name)
+
         za_transpose(0, 0, 0)
         za_transpose(0, 0, 1)
-        for t in range(PACK):
-            widen_w(0, 0, t)
         zr_interleave(0, 0, 0, "delta_bank_0")
         zr_interleave(0, 0, 1, "delta_bank_2")
         za_scale(0, 0, 0)
@@ -302,80 +323,85 @@ def tile_coupledlstmfoldedweightgradient_kernel(tc, z, c, w_bytes, w_scale, b, a
         zr_scale(0, 0, 0)
         za_quantize(0, 0)
         zr_scale(0, 0, 1)
+        for span, t in ((0, 0), (0, 1), (1, 0), (1, 1), (0, 2), (0, 3)):
+            widen_w(span, 0, t)
         zr_interleave(0, 1, 0, "delta_bank_0")
+        first_w_tensor((0, 1), "p_bank_2")
+        first_w_tensor((2,), "cd_bank")
         zr_interleave(0, 1, 1, "delta_bank_2")
-        for gate in range(GATES):
-            interleave_w_vector(0, 0, gate)
         for t in range(PACK):
             widen_w(0, 1, t)
+        first_w_copy((0, 1))
+        first_w_copy((2,))
         za_scale(0, 1, 0)
         za_scale(0, 1, 1)
         bias_bank = psum.tile([P, P], BF16, name="cd_bank")
         nc.tensor.transpose(bias_bank[:], bias_rows[:], ident_bf16[:])
         za_transpose(1, 0, 0)
         za_transpose(1, 0, 1)
-        interleave_w_vector(0, 1, 0)
+        zr_quantize(0, 0)
+        zr_scale(0, 1, 0)
         za_quantize(0, 1)
+        interleave_w_vector(0, 1, 0)
         interleave_w_vector(0, 1, 1)
+        zr_scale(0, 1, 1)
         quantize_w(0, 0, 1)
         preact(0, 0)
-        bias_sb = keep.tile([P, GATES * TILES], F32)
-        nc.vector.tensor_copy(out=bias_sb[:], in_=bias_bank[:, 0:GATES * TILES])
         interleave_w_vector(0, 1, 2)
         quantize_w(0, 1, 1)
         preact(0, 1)
+        bias_sb = keep.tile([P, GATES * TILES], F32)
+        nc.vector.tensor_copy(out=bias_sb[:], in_=bias_bank[:, 0:GATES * TILES])
         za_scale(1, 0, 0)
         quantize_w(0, 2, 1)
         preact(0, 2)
         cd_transpose(0)
-        for g in range(PASSES):
-            for t in range(PACK):
-                widen_w(1, g, t)
+        for span, g, t in ((1, 0, 2), (1, 0, 3), (1, 1, 0), (1, 1, 1)):
+            widen_w(span, g, t)
         za_scale(1, 0, 1)
         za_transpose(1, 1, 0)
         za_transpose(1, 1, 1)
-        zr_quantize(0, 0)
-        zr_scale(0, 1, 0)
+        zr_quantize(0, 1)
         za_quantize(1, 0)
-        zr_scale(0, 1, 1)
         gate_act(0, GATE_F)
         gate_act(0, GATE_G)
+        widen_w(1, 1, 2)
+        widen_w(1, 1, 3)
         gate_act(0, GATE_O)
-        act("g2", ACT.Square, "g", 0, 3)
-
-        za_scale(1, 1, 0)
-        za_scale(1, 1, 1)
-        interleave_w_tensor(1, 0)
-        interleave_w_tensor(1, 1)
-        op_d(0)
-        za_quantize(1, 1)
-        for gate in (GATE_G, GATE_F, GATE_O):
-            preact(1, gate)
         widen_w(2, 0, 0)
         widen_w(2, 0, 1)
-        w_copy(1, 0)
-        w_copy(1, 1)
-        zr_interleave(1, 0, 0, "delta_bank_0")
-        interleave_w_tensor(1, 2)
-        widen_w(2, 0, 2)
+
+        op_d(0)
+        za_scale(1, 1, 0)
         tt("fd", "f", "d", ALU.mult, 0)
-        op_na(0)
-        tt("cn", "fd", "g", ALU.add, 0)
+        za_scale(1, 1, 1)
+        zr_interleave(1, 0, 0, "delta_bank_0")
         zr_interleave(1, 0, 1, "delta_bank_2")
+        tt("cn", "fd", "g", ALU.add, 0)
+        za_quantize(1, 1)
+        preact(1, GATE_G)
+        preact(1, GATE_F)
+        interleave_w_tensor(1, 0)
+        op_na(0)
         cd_transpose(1)
+        interleave_w_tensor(1, 1)
+        preact(1, GATE_O)
+        act("tc", ACT.Tanh, "cn", 0)
+        act("g2", ACT.Square, "g", 0, 3)
+        act("s", ACT.Square, "tc", 0)
         gate_act(1, GATE_G)
         gate_act(1, GATE_F)
-        act("tc", ACT.Tanh, "cn", 0)
-        w_copy(1, 2)
-        act("s", ACT.Square, "tc", 0)
+        w_copy(1, 0)
+        interleave_w_tensor(1, 2)
+        w_copy(1, 1)
         gate_act(1, GATE_O)
+        w_copy(1, 2)
         act("g2", ACT.Square, "g", 1, 3)
-        widen_w(2, 0, 3)
-        zr_quantize(0, 1)
-        quantize_w(1, 0, 2)
         zr_scale(1, 0, 0)
-        quantize_w(1, 2, 1)
+        tt("nm", "na", "tc", ALU.mult, 0)
         zr_scale(1, 0, 1)
+        widen_w(2, 0, 2, True)
+        widen_w(2, 0, 3, True)
 
         def zr_job(s, g, half):
             return (lambda: zr_interleave(s, g, half), lambda: zr_scale(s, g, half))
@@ -391,24 +417,27 @@ def tile_coupledlstmfoldedweightgradient_kernel(tc, z, c, w_bytes, w_scale, b, a
 
         idle = (lambda: None, lambda: None)
         jobs = {
-            1: [zr_job(1, 1, 0), zr_job(1, 1, 1), idle, w_job(2, 0)],
-            2: [w_job(2, 1), w_job(2, 2), w_job(3, 0), w_job(3, 1)],
-            3: out_jobs(0)[:2] + [w_job(3, 2), out_jobs(0)[2]],
-            4: out_jobs(0)[3:] + [idle],
-            5: out_jobs(1)[:3] + [idle],
-            6: out_jobs(1)[3:] + [idle],
+            1: [zr_job(1, 1, 0), zr_job(1, 1, 1), idle, idle, idle],
+            2: [w_job(2, 0), w_job(2, 1), w_job(2, 2), w_job(3, 0), idle],
+            3: out_jobs(0)[:2] + [w_job(3, 1), out_jobs(0)[2], idle],
+            4: out_jobs(0)[3:5] + [w_job(3, 2), out_jobs(0)[5], idle],
+            5: out_jobs(1)[:3] + [idle, idle],
+            6: out_jobs(1)[3:] + [idle, idle],
         }
+        widen_plan = {1: ([(1, 0), (1, 1)], [(1, 2), (1, 3)])}
 
         for i in range(1, UNITS - 1):
             old = i >= 2
             if old:
                 delta_copy(fg(i - 2))
-            for gate in (GATE_G, GATE_F, GATE_O):
-                preact(i + 1, gate)
+                jobs[i - 1][4][1]()
+            for g, t in widen_plan.get(i, ([], []))[0]:
+                widen_w(2, g, t)
             stt(new("dct", i - 1), "s", 1.0, ALU.subtract, "na", i - 1)
             if i == 1:
-                for t in range(2):
-                    widen_w(2, 1, t)
+                quantize_w(1, 0, 2)
+            preact(i + 1, GATE_G)
+            preact(i + 1, GATE_F)
             op_d(i)
             if old:
                 delta_quantize(one(GATE_O, i - 2))
@@ -417,50 +446,43 @@ def tile_coupledlstmfoldedweightgradient_kernel(tc, z, c, w_bytes, w_scale, b, a
             jobs[i][0][0]()
             jobs[i][1][0]()
             stt(new("nq", i - 1), "f", 1.0, ALU.subtract, "dct", i - 1)
+            if i % 2 == 1:
+                quantize_w(i // 2 + 1, 2, 1)
+            preact(i + 1, GATE_O)
             tt("fd", "f", "d", ALU.mult, i)
             if old:
                 delta_quantize(fg(i - 2))
-            tt("nm", "na", "tc", ALU.mult, i - 1)
+                tt("nm", "na", "tc", ALU.mult, i - 1)
             gate_act(i + 1, GATE_G)
-            gate_act(i + 1, GATE_F)
             jobs[i][0][1]()
+            gate_act(i + 1, GATE_F)
             tt("cn", "fd", "g", ALU.add, i)
             jobs[i][1][1]()
             jobs[i][2][0]()
             act("tc", ACT.Tanh, "cn", i)
             gate_act(i + 1, GATE_O)
             act("s", ACT.Square, "tc", i)
-            stt(new_delta(GATE_O, i - 1), "o", 1.0, ALU.subtract, "nm", i - 1)
+            finish(GATE_O, i - 1, None)
             delta_transpose(one(GATE_O, i - 1), "delta_bank_2")
             op_na(i)
             cd_transpose(i + 1)
-            act("g2", ACT.Square, "g", i + 1, 3)
             delta_copy(one(GATE_O, i - 1))
-            if i == 1:
-                for t in range(2, PACK):
-                    widen_w(2, 1, t)
             jobs[i][3][0]()
-            stt(new_delta(GATE_F, i - 1), "nq", -1.0, ALU.mult, "fd", i - 1)
             jobs[i][2][1]()
-            stt(new_delta(GATE_G, i - 1), "g2", 1.0, ALU.subtract, "nq", i - 1)
+            act("g2", ACT.Square, "g", i + 1, 3)
+            finish(GATE_F, i - 1, None)
+            finish(GATE_G, i - 1, None)
             delta_transpose(fg(i - 1), "delta_bank_0")
+            jobs[i][4][0]()
             jobs[i][3][1]()
+            for g, t in widen_plan.get(i, ([], []))[1]:
+                widen_w(2, g, t)
             if i == 1:
                 zr_quantize(1, 1)
             if i in (2, 4):
                 quantize_w(i // 2 + 1, 0, 2)
-                quantize_w(i // 2 + 1, 2, 1)
 
         last, prev, j = UNITS - 1, UNITS - 2, TILES - 1
-
-        def finish(gate, i, bank_name):
-            if gate == GATE_F:
-                stt(new_delta(gate, i), "nq", -1.0, ALU.mult, "fd", i)
-            elif gate == GATE_G:
-                stt(new_delta(gate, i), "g2", 1.0, ALU.subtract, "nq", i)
-            else:
-                stt(new_delta(gate, i), "o", 1.0, ALU.subtract, "nm", i)
-            delta_transpose(one(gate, i), bank_name)
 
         delta_copy(fg(prev - 1))
         op_d(last)

from contextlib import ExitStack

import concourse.mybir as mybir
from concourse.masks import make_identity

N, K, H = 1024, 1024, 512
GATES = 3
FLOPS = 2 * 2 * N * K * GATES * H

F32 = mybir.dt.float32
BF16 = mybir.dt.bfloat16
U32 = mybir.dt.uint32
U8 = mybir.dt.uint8
FP8 = mybir.dt.float8_e4m3fn
FP8X4 = mybir.dt.float8_e4m3fn_x4
ALU = mybir.AluOpType
ACT = mybir.ActivationFunctionType

P = 128
PACK = 4
PASS = P * PACK
PASSES = 2
TILES = H // P
UNITS = TILES * PASSES
GATE_F, GATE_G, GATE_O = 0, 1, 2
WIDEN_SPANS = [(0, 1), (1, 1), (2, 2)]


def tile_coupledlstmfoldedweightgradient_kernel(tc, z, c, w_bytes, w_scale, b, a, r, dh_new, out):
    nc = tc.nc
    with ExitStack() as ctx:
        keep = ctx.enter_context(tc.tile_pool(name="keep", bufs=1))
        work = ctx.enter_context(tc.tile_pool(name="work", bufs=2))
        psum = ctx.enter_context(tc.psum_pool(name="psum", bufs=1))
        ctx.enter_context(tc.manual_schedule())

        def quantize(codes, scales, values):
            nc.vector.quantize_mx(out=codes.bitcast(FP8X4), scales=scales, in_=values)

        def mx_tiles(pool, name, width, bufs=None):
            codes = pool.tile([P, width], U32, name=name + "_codes", bufs=bufs, align_bytes=64)
            scales = pool.tile([P, width], U8, name=name + "_scales", bufs=bufs, align_bytes=64)
            return codes, scales

        def matmul_mx(acc, lhs, lhs_cols, rhs, rhs_cols, start, stop):
            nc.tensor.matmul_mx(
                out=acc, lhsT=lhs[0][:, lhs_cols].bitcast(FP8X4), lhsT_scale=lhs[1][:, lhs_cols],
                rhs=rhs[0][:, rhs_cols].bitcast(FP8X4), rhs_scale=rhs[1][:, rhs_cols], start=start, stop=stop)

        def spare_bank(shape, dtype, borrow=None):
            if borrow:
                return psum.tile(shape, dtype, name=borrow)
            return psum.tile(shape, dtype, name="spare_bank", bufs=2)

        ident_f32 = keep.tile([P, P], F32)
        make_identity(nc, ident_f32[:])
        ident_bf16 = keep.tile([P, P], BF16)
        make_identity(nc, ident_bf16[:])
        bias_rows = keep.tile([P, P], BF16)
        nc.gpsimd.memset(bias_rows[:], 0.0)
        warm_in = keep.tile([P, 1], F32)
        nc.vector.memset(warm_in[:], 0.0)
        warm_out = keep.tile([P, 1], F32)
        nc.scalar.activation(out=warm_out[:], in_=warm_in[:], func=ACT.Sigmoid)

        z_sb, w_raw, c_sb, dh_sb = {}, {}, {}, {}

        def load_z(s, g, parts=1):
            z_sb[s, g] = keep.tile([P, PACK, PASS], BF16, name="z_%d_%d" % (s, g))
            rows = z[s * PASS:(s + 1) * PASS, g * PASS:(g + 1) * PASS]
            words = rows.rearrange("(p t) k -> p t k", t=PACK).bitcast(F32)
            for part in range(parts):
                span = slice(part * PACK // parts, (part + 1) * PACK // parts)
                nc.sync.dma_start(out=z_sb[s, g][:].bitcast(F32)[:, span, :], in_=words[:, span, :])

        def load_w(g, half):
            w_raw[g, half] = keep.tile([P, 2, GATES * H], U8, name="w_raw_%d_%d" % (g, half))
            rows = w_bytes[g * PASS:(g + 1) * PASS, :].rearrange("(p t) n -> p t n", t=PACK)
            nc.sync.dma_start(out=w_raw[g, half][:], in_=rows[:, 2 * half:2 * half + 2, :])

        def load_tokens(tiles, name, src, s):
            tiles[s] = keep.tile([P, PACK, H], BF16, name="%s_%d" % (name, s))
            nc.sync.dma_start(out=tiles[s][:], in_=src[s * PASS:(s + 1) * PASS, :].rearrange("(p t) h -> p t h", t=PACK))

        a_sb = keep.tile([P, PASSES, PACK], BF16)
        nc.sync.dma_start(out=a_sb[:], in_=a.rearrange("(g p t) -> p g t", p=P, t=PACK))
        load_z(0, 0, 2)
        scale_sb = keep.tile([P, PASSES, PACK], F32)
        nc.sync.dma_start(out=scale_sb[:], in_=w_scale.rearrange("(g p t) o -> p g (t o)", p=P, t=PACK))
        load_w(0, 0)
        r_sb = keep.tile([P, PASSES, PACK], BF16)
        nc.sync.dma_start(out=r_sb[:], in_=r.rearrange("(s p t) -> p s t", p=P, t=PACK))
        load_z(0, 1)
        load_w(0, 1)
        load_w(1, 0)
        load_w(1, 1)
        nc.sync.dma_start(out=bias_rows[0:GATES * TILES, :], in_=b.rearrange("(x p) -> x p", p=P))
        load_z(1, 0)
        load_tokens(c_sb, "c", c, 0)
        load_tokens(dh_sb, "dh", dh_new, 0)
        load_z(1, 1)
        load_tokens(c_sb, "c", c, 1)
        load_tokens(dh_sb, "dh", dh_new, 1)

        a_twice = keep.tile([P, PASSES, 2, PACK], BF16)
        nc.gpsimd.tensor_copy(out=a_twice[:], in_=a_sb[:].unsqueeze(2).to_broadcast([P, PASSES, 2, PACK]))

        w_wide, w_grouped, w_mx, w_bank = {}, {}, {}, {}

        def widen_w(span, g, t, on_vector=False):
            first, count = WIDEN_SPANS[span]
            if t == 0:
                w_wide[span, g] = keep.tile([P, PACK, GATES, count * P], BF16, name="w_wide_%d_%d" % (span, g))
            for gate in range(GATES):
                col = gate * H + first * P
                dst = w_wide[span, g][:, t, gate, :]
                src = w_raw[g, t // 2][:, t % 2, col:col + count * P].bitcast(FP8)
                if on_vector:
                    nc.vector.tensor_scalar(out=dst, in0=src, scalar1=scale_sb[:, g, t:t + 1], scalar2=None, op0=ALU.mult)
                else:
                    nc.scalar.activation(out=dst, in_=src, func=ACT.Copy, scale=scale_sb[:, g, t:t + 1])

        def wide_slice(j, g, gate):
            span = min(j, len(WIDEN_SPANS) - 1)
            col = (j - WIDEN_SPANS[span][0]) * P
            return w_wide[span, g][:, :, gate, col:col + P]

        def grouped_w(j):
            if j not in w_grouped:
                w_grouped[j] = work.tile([P, GATES, PASSES, P, PACK], BF16, name="w_grouped", align_bytes=64)
                w_mx[j] = mx_tiles(keep, "w_%d" % j, GATES * PASSES * P)
            return w_grouped[j]

        def interleave_w_vector(j, g, gate):
            nc.vector.tensor_copy(
                out=grouped_w(j)[:, gate, g, :, :].rearrange("p (n i) t -> p n t i", i=4),
                in_=wide_slice(j, g, gate).rearrange("p t (n i) -> p n t i", i=4))

        def interleave_w_tensor(j, gate):
            bank = spare_bank([P, PASSES, P, PACK], BF16)
            for g in range(PASSES):
                nc.tensor.matmul(out=bank[:, g, :, :].rearrange("p n t -> p t n"), lhsT=ident_bf16[:],
                                 rhs=wide_slice(j, g, gate), start=True, stop=True)
            w_bank[j, gate] = bank

        def first_w_tensor(gates, borrow):
            bank = spare_bank([P, len(gates), P, PACK], BF16, borrow)
            for x, gate in enumerate(gates):
                nc.tensor.matmul(out=bank[:, x, :, :].rearrange("p n t -> p t n"), lhsT=ident_bf16[:],
                                 rhs=wide_slice(0, 0, gate), start=True, stop=True)
            w_bank[0, gates] = bank

        def first_w_copy(gates):
            nc.scalar.copy(out=grouped_w(0)[:, gates[0]:gates[-1] + 1, 0, :, :], in_=w_bank[0, gates][:])

        def w_copy(j, gate):
            nc.scalar.copy(out=grouped_w(j)[:, gate, :, :, :], in_=w_bank[j, gate][:])

        def quantize_w(j, gate, count):
            cols = slice(gate * PASSES * P, (gate + count) * PASSES * P)
            quantize(w_mx[j][0][:, cols], w_mx[j][1][:, cols],
                     w_grouped[j][:, gate:gate + count].rearrange("p x g n t -> p (x g n t)"))

        za_grouped, za_mx, za_bank = {}, {}, {}

        def za_transpose(s, g, u):
            bank = spare_bank([P, 4, P], F32)
            words = z_sb[s, g][:].bitcast(F32)
            for e in range(2):
                for v in range(2):
                    nc.tensor.transpose(bank[:, 2 * e + v, :], words[:, 2 * u + e, v:PASS // 2:2], ident_f32[:])
            za_bank[s, g, u] = bank

        def za_scale(s, g, u):
            if u == 0:
                za_grouped[s, g] = work.tile([P, 2, P * 8], BF16, name="za_grouped", align_bytes=64)
            gain = a_twice[:, g].rearrange("p e (v i) -> p (e v) i", i=2)
            nc.vector.tensor_tensor(
                out=za_grouped[s, g][:, u, :].rearrange("p (q x i) -> p q x i", x=4, i=2),
                in0=za_bank[s, g, u][:].bitcast(BF16).rearrange("p x (q i) -> p q x i", i=2),
                in1=gain.unsqueeze(1).to_broadcast([P, P, 4, 2]), op=ALU.mult)

        def za_quantize(s, g):
            za_mx[s, g] = mx_tiles(keep, "za_%d_%d" % (s, g), PASS)
            quantize(za_mx[s, g][0][:], za_mx[s, g][1][:], za_grouped[s, g][:].rearrange("p u n -> p (u n)"))

        zr_grouped, zr_mx, zr_bank = {}, {}, {}

        def zr_interleave(s, g, half, borrow=None):
            bank = spare_bank([P, 2, P, PACK], BF16, borrow)
            for m in range(2):
                col = (2 * half + m) * P
                nc.tensor.matmul(out=bank[:, m, :, :].rearrange("p n t -> p t n"), lhsT=ident_bf16[:],
                                 rhs=z_sb[s, g][:, :, col:col + P], start=True, stop=True)
            zr_bank[s, g, half] = bank

        def zr_scale(s, g, half):
            if half == 0:
                zr_grouped[s, g] = work.tile([P, 2, 2 * P, PACK], BF16, name="zr_grouped", align_bytes=64)
            nc.vector.tensor_tensor(
                out=zr_grouped[s, g][:, half], in0=zr_bank[s, g, half][:].rearrange("p m n t -> p (m n) t"),
                in1=r_sb[:, s, :].unsqueeze(1).to_broadcast([P, 2 * P, PACK]), op=ALU.mult)

        def zr_quantize(s, g):
            zr_mx[s, g] = mx_tiles(keep, "zr_%d_%d" % (s, g), PASS)
            quantize(zr_mx[s, g][0][:], zr_mx[s, g][1][:], zr_grouped[s, g][:].rearrange("p h n t -> p (h n t)"))

        val = {}

        def new(name, i, bufs=2):
            val[name, i] = work.tile([P, PASS], F32, name=name, bufs=bufs)
            return val[name, i][:]

        def preact(i, gate):
            j, s = divmod(i, PASSES)
            bank = psum.tile([P, PASS], F32, name="p_bank_%d" % gate)
            for g in range(PASSES):
                col = (gate * PASSES + g) * P
                matmul_mx(bank[:], w_mx[j], slice(col, col + P), za_mx[s, g], slice(0, PASS), g == 0, g == PASSES - 1)
            val["p", gate, i] = bank

        def gate_act(i, gate):
            name, func, bufs = [("f", ACT.Sigmoid, 3), ("g", ACT.Tanh, 2), ("o", ACT.Sigmoid, 3)][gate]
            col = gate * TILES + i // PASSES
            nc.scalar.activation(out=new(name, i, bufs), in_=val["p", gate, i][:], func=func, bias=bias_sb[:, col:col + 1])

        def act(name, func, src, i, bufs=2):
            nc.scalar.activation(out=new(name, i, bufs), in_=val[src, i][:], func=func)

        def cd_transpose(i):
            j, s = divmod(i, PASSES)
            bank = psum.tile([P, 2, PACK, P], BF16, name="cd_bank")
            for x, src in enumerate((c_sb, dh_sb)):
                for t in range(PACK):
                    nc.tensor.transpose(bank[:, x, t, :], src[s][:, t, j * P:(j + 1) * P], ident_bf16[:])
            val["cd", i] = bank

        def tt(name, x, y, op, i):
            nc.vector.tensor_tensor(out=new(name, i), in0=val[x, i][:], in1=val[y, i][:], op=op)

        def stt(dst, x, scalar, op0, y, i):
            nc.vector.scalar_tensor_tensor(out=dst, in0=val[x, i][:], scalar=scalar, in1=val[y, i][:], op0=op0, op1=ALU.mult)

        def op_d(i):
            nc.vector.tensor_tensor(
                out=new("d", i).rearrange("p (u q e) -> p u q e", u=2, e=2),
                in0=val["cd", i][:, 0].rearrange("p (u e) q -> p u q e", e=2),
                in1=val["g", i][:].rearrange("p (u q e) -> p u q e", u=2, e=2), op=ALU.subtract)

        def op_na(i):
            dst = new("na", i).rearrange("p (u q e) -> p u q e", u=2, e=2)
            for u in range(2):
                nc.vector.scalar_tensor_tensor(
                    out=dst[:, u], in0=val["cd", i][:, 1, 2 * u:2 * u + 2, :].rearrange("p e q -> p q e"), scalar=-1.0,
                    in1=val["o", i][:].rearrange("p (u q e) -> p u q e", u=2, e=2)[:, u], op0=ALU.mult, op1=ALU.mult)

        def new_delta(gate, i):
            val["delta", gate, i] = work.tile([P, PASS], BF16, name="delta_%d" % gate)
            return val["delta", gate, i][:]

        def delta_transpose(items, bank_name):
            bank = psum.tile([P, len(items), 2, P], F32, name=bank_name)
            for x, item in enumerate(items):
                words = val[("delta",) + item][:].bitcast(F32)
                for u in range(2):
                    nc.tensor.transpose(bank[:, x, u, :], words[:, u * P:(u + 1) * P], ident_f32[:])
            val["dbank", items] = bank

        def delta_copy(items):
            grouped = work.tile([P, len(items) * PASS], BF16, name="delta_grouped_%d" % len(items), bufs=3, align_bytes=64)
            nc.scalar.copy(out=grouped[:].bitcast(F32).rearrange("p (x h u) -> p x h u", h=P, u=2),
                           in_=val["dbank", items][:].rearrange("p x u h -> p x h u"))
            val["dgrouped", items] = grouped

        def delta_quantize(items):
            tiles = mx_tiles(work, "delta_%d" % len(items), len(items) * P, bufs=5)
            quantize(tiles[0][:], tiles[1][:], val["dgrouped", items][:])
            for x, item in enumerate(items):
                val[("dmx",) + item] = (tiles, slice(x * P, (x + 1) * P))

        def fg(i):
            return ((GATE_F, i), (GATE_G, i))

        def one(gate, i):
            return ((gate, i),)

        def out_matmul(j, gate, g, borrow=None, first=0, count=4):
            bank = spare_bank([P, count, P], F32, borrow)
            for x in range(count):
                m = first + x
                for s in range(PASSES):
                    tiles, cols = val["dmx", gate, j * PASSES + s]
                    matmul_mx(bank[:, x, :], zr_mx[s, g], slice(m * P, (m + 1) * P), tiles, cols, s == 0, s == PASSES - 1)
            val["obank", j, gate, g, first] = bank

        def out_store(j, gate, g, on_vector=False, first=0, count=4):
            stage = work.tile([P, count, P], F32, name="stage_%d" % count, bufs=4 if count == 4 else 8)
            copy = nc.vector.tensor_copy if on_vector else nc.scalar.copy
            copy(out=stage[:], in_=val["obank", j, gate, g, first][:])
            row, col = g * PASS + first * P, gate * H + j * P
            nc.sync.dma_start(out=out[row:row + count * P, col:col + P].rearrange("(m p) n -> p m n", p=P), in_=stage[:])

        FG, O = (GATE_F, GATE_G), (GATE_O,)

        def finish(gate, i, bank_name):
            if gate == GATE_F:
                stt(new_delta(gate, i), "nq", -1.0, ALU.mult, "fd", i)
            elif gate == GATE_G:
                stt(new_delta(gate, i), "g2", 1.0, ALU.subtract, "nq", i)
            else:
                stt(new_delta(gate, i), "o", 1.0, ALU.subtract, "nm", i)
            if bank_name:
                delta_transpose(one(gate, i), bank_name)

        za_transpose(0, 0, 0)
        za_transpose(0, 0, 1)
        zr_interleave(0, 0, 0, "delta_bank_0")
        zr_interleave(0, 0, 1, "delta_bank_2")
        za_scale(0, 0, 0)
        za_scale(0, 0, 1)
        za_transpose(0, 1, 0)
        za_transpose(0, 1, 1)
        zr_scale(0, 0, 0)
        za_quantize(0, 0)
        zr_scale(0, 0, 1)
        for span, t in ((0, 0), (0, 1), (1, 0), (1, 1), (0, 2), (0, 3)):
            widen_w(span, 0, t)
        zr_interleave(0, 1, 0, "delta_bank_0")
        first_w_tensor((0, 1), "p_bank_2")
        first_w_tensor((2,), "cd_bank")
        zr_interleave(0, 1, 1, "delta_bank_2")
        for t in range(PACK):
            widen_w(0, 1, t)
        first_w_copy((0, 1))
        first_w_copy((2,))
        za_scale(0, 1, 0)
        za_scale(0, 1, 1)
        bias_bank = psum.tile([P, P], BF16, name="cd_bank")
        nc.tensor.transpose(bias_bank[:], bias_rows[:], ident_bf16[:])
        za_transpose(1, 0, 0)
        za_transpose(1, 0, 1)
        zr_quantize(0, 0)
        zr_scale(0, 1, 0)
        za_quantize(0, 1)
        interleave_w_vector(0, 1, 0)
        interleave_w_vector(0, 1, 1)
        zr_scale(0, 1, 1)
        quantize_w(0, 0, 1)
        preact(0, 0)
        interleave_w_vector(0, 1, 2)
        quantize_w(0, 1, 1)
        preact(0, 1)
        bias_sb = keep.tile([P, GATES * TILES], F32)
        nc.vector.tensor_copy(out=bias_sb[:], in_=bias_bank[:, 0:GATES * TILES])
        za_scale(1, 0, 0)
        quantize_w(0, 2, 1)
        preact(0, 2)
        cd_transpose(0)
        for span, g, t in ((1, 0, 2), (1, 0, 3), (1, 1, 0), (1, 1, 1)):
            widen_w(span, g, t)
        za_scale(1, 0, 1)
        za_transpose(1, 1, 0)
        za_transpose(1, 1, 1)
        zr_quantize(0, 1)
        za_quantize(1, 0)
        gate_act(0, GATE_F)
        gate_act(0, GATE_G)
        widen_w(1, 1, 2)
        widen_w(1, 1, 3)
        gate_act(0, GATE_O)
        widen_w(2, 0, 0)
        widen_w(2, 0, 1)

        op_d(0)
        za_scale(1, 1, 0)
        tt("fd", "f", "d", ALU.mult, 0)
        za_scale(1, 1, 1)
        zr_interleave(1, 0, 0, "delta_bank_0")
        zr_interleave(1, 0, 1, "delta_bank_2")
        tt("cn", "fd", "g", ALU.add, 0)
        za_quantize(1, 1)
        preact(1, GATE_G)
        preact(1, GATE_F)
        interleave_w_tensor(1, 0)
        op_na(0)
        cd_transpose(1)
        interleave_w_tensor(1, 1)
        preact(1, GATE_O)
        act("tc", ACT.Tanh, "cn", 0)
        act("g2", ACT.Square, "g", 0, 3)
        act("s", ACT.Square, "tc", 0)
        gate_act(1, GATE_G)
        gate_act(1, GATE_F)
        w_copy(1, 0)
        interleave_w_tensor(1, 2)
        w_copy(1, 1)
        gate_act(1, GATE_O)
        w_copy(1, 2)
        act("g2", ACT.Square, "g", 1, 3)
        zr_scale(1, 0, 0)
        tt("nm", "na", "tc", ALU.mult, 0)
        zr_scale(1, 0, 1)
        widen_w(2, 0, 2, True)
        widen_w(2, 0, 3, True)

        def zr_job(s, g, half):
            return (lambda: zr_interleave(s, g, half), lambda: zr_scale(s, g, half))

        def w_job(j, gate):
            return (lambda: interleave_w_tensor(j, gate), lambda: w_copy(j, gate))

        def out_job(j, gate, g, on_vector=False):
            return (lambda: out_matmul(j, gate, g), lambda: out_store(j, gate, g, on_vector))

        def out_jobs(j):
            return [out_job(j, gate, g) for gate in (GATE_O, GATE_F, GATE_G) for g in range(PASSES)]

        idle = (lambda: None, lambda: None)
        jobs = {
            1: [zr_job(1, 1, 0), zr_job(1, 1, 1), idle, idle, idle],
            2: [w_job(2, 0), w_job(2, 1), w_job(2, 2), w_job(3, 0), idle],
            3: out_jobs(0)[:2] + [w_job(3, 1), out_jobs(0)[2], idle],
            4: out_jobs(0)[3:5] + [w_job(3, 2), out_jobs(0)[5], idle],
            5: out_jobs(1)[:3] + [idle, idle],
            6: out_jobs(1)[3:] + [idle, idle],
        }
        widen_plan = {1: ([(1, 0), (1, 1)], [(1, 2), (1, 3)])}

        for i in range(1, UNITS - 1):
            old = i >= 2
            if old:
                delta_copy(fg(i - 2))
                jobs[i - 1][4][1]()
            for g, t in widen_plan.get(i, ([], []))[0]:
                widen_w(2, g, t)
            stt(new("dct", i - 1), "s", 1.0, ALU.subtract, "na", i - 1)
            if i == 1:
                quantize_w(1, 0, 2)
            preact(i + 1, GATE_G)
            preact(i + 1, GATE_F)
            op_d(i)
            if old:
                delta_quantize(one(GATE_O, i - 2))
            else:
                zr_quantize(1, 0)
            jobs[i][0][0]()
            jobs[i][1][0]()
            stt(new("nq", i - 1), "f", 1.0, ALU.subtract, "dct", i - 1)
            if i % 2 == 1:
                quantize_w(i // 2 + 1, 2, 1)
            preact(i + 1, GATE_O)
            tt("fd", "f", "d", ALU.mult, i)
            if old:
                delta_quantize(fg(i - 2))
                tt("nm", "na", "tc", ALU.mult, i - 1)
            gate_act(i + 1, GATE_G)
            jobs[i][0][1]()
            gate_act(i + 1, GATE_F)
            tt("cn", "fd", "g", ALU.add, i)
            jobs[i][1][1]()
            jobs[i][2][0]()
            act("tc", ACT.Tanh, "cn", i)
            gate_act(i + 1, GATE_O)
            act("s", ACT.Square, "tc", i)
            finish(GATE_O, i - 1, None)
            delta_transpose(one(GATE_O, i - 1), "delta_bank_2")
            op_na(i)
            cd_transpose(i + 1)
            delta_copy(one(GATE_O, i - 1))
            jobs[i][3][0]()
            jobs[i][2][1]()
            act("g2", ACT.Square, "g", i + 1, 3)
            finish(GATE_F, i - 1, None)
            finish(GATE_G, i - 1, None)
            delta_transpose(fg(i - 1), "delta_bank_0")
            jobs[i][4][0]()
            jobs[i][3][1]()
            for g, t in widen_plan.get(i, ([], []))[1]:
                widen_w(2, g, t)
            if i == 1:
                zr_quantize(1, 1)
            if i in (2, 4):
                quantize_w(i // 2 + 1, 0, 2)

        last, prev, j = UNITS - 1, UNITS - 2, TILES - 1

        delta_copy(fg(prev - 1))
        op_d(last)
        delta_quantize(one(GATE_O, prev - 1))
        out_matmul(j - 1, GATE_O, 0)
        out_matmul(j - 1, GATE_O, 1)
        tt("nm", "na", "tc", ALU.mult, prev)
        tt("fd", "f", "d", ALU.mult, last)
        delta_quantize(fg(prev - 1))
        out_matmul(j - 1, GATE_F, 0, "p_bank_0")
        out_matmul(j - 1, GATE_F, 1, "p_bank_1")
        out_store(j - 1, GATE_O, 0)
        out_store(j - 1, GATE_O, 1)
        finish(GATE_O, prev, "delta_bank_2")
        out_matmul(j - 1, GATE_G, 0, "p_bank_2")
        out_matmul(j - 1, GATE_G, 1)
        tt("cn", "fd", "g", ALU.add, last)
        out_store(j - 1, GATE_F, 0)
        act("tc", ACT.Tanh, "cn", last)
        delta_copy(one(GATE_O, prev))
        act("s", ACT.Square, "tc", last)
        out_store(j - 1, GATE_F, 1)
        out_store(j - 1, GATE_G, 0)
        stt(new("dct", prev), "s", 1.0, ALU.subtract, "na", prev)
        op_na(last)
        stt(new("nq", prev), "f", 1.0, ALU.subtract, "dct", prev)
        tt("nm", "na", "tc", ALU.mult, last)
        delta_quantize(one(GATE_O, prev))
        finish(GATE_O, last, "delta_bank_2")
        delta_copy(one(GATE_O, last))
        out_store(j - 1, GATE_G, 1)
        stt(new("dct", last), "s", 1.0, ALU.subtract, "na", last)
        finish(GATE_F, prev, "delta_bank_0")
        delta_copy(one(GATE_F, prev))
        delta_quantize(one(GATE_O, last))
        out_matmul(j, GATE_O, 0, "p_bank_0")
        out_matmul(j, GATE_O, 1, "p_bank_1")
        stt(new("nq", last), "f", 1.0, ALU.subtract, "dct", last)
        delta_quantize(one(GATE_F, prev))
        finish(GATE_F, last, "delta_bank_0")
        out_store(j, GATE_O, 0)
        out_store(j, GATE_O, 1)
        delta_copy(one(GATE_F, last))
        finish(GATE_G, prev, "cd_bank")
        delta_copy(one(GATE_G, prev))
        finish(GATE_G, last, "delta_bank_2")
        delta_quantize(one(GATE_F, last))
        delta_copy(one(GATE_G, last))
        delta_quantize(one(GATE_G, prev))
        halves = [(g, first) for g in range(PASSES) for first in (0, 2)]
        for (g, first), bank_name in zip(halves, (None, None, "p_bank_2", "p_bank_0")):
            out_matmul(j, GATE_F, g, bank_name, first, 2)
        delta_quantize(one(GATE_G, last))
        for x, (g, first) in enumerate(halves):
            out_store(j, GATE_F, g, x % 2 == 1, first, 2)
        for (g, first), bank_name in zip(halves, ("p_bank_1", "cd_bank", "delta_bank_0", "delta_bank_2")):
            out_matmul(j, GATE_G, g, bank_name, first, 2)
        for x, (g, first) in enumerate(halves):
            out_store(j, GATE_G, g, x % 2 == 1, first, 2)
